import numpy as np
import ml_dtypes


def mxq(x, axis, fmt="e4m3"):
    dtype, down = {"e4m3": (ml_dtypes.float8_e4m3fn, 7), "e5m2": (ml_dtypes.float8_e5m2, 14)}[fmt]
    v = np.moveaxis(np.asarray(x, np.float32).astype(ml_dtypes.bfloat16).astype(np.float64), axis, -1)
    blocks = v.reshape(v.shape[:-1] + (-1, 32))
    amax = np.abs(blocks).max(-1, keepdims=True)
    byte = np.maximum(np.where(amax > 0, np.frexp(amax)[1] - 1 + 127, 0) - down, 1)
    scale = np.exp2(byte - 127.0)
    codes = (blocks / scale).astype(np.float32).astype(dtype).astype(np.float64)
    return np.moveaxis((codes * scale).reshape(v.shape), -1, axis)


WIDE = False


def mx_kscale(k):
    if not WIDE:
        return np.ones(k)
    levels = np.array([10, -10, 5, -5, 0])
    if k % 512:
        return np.exp2(np.random.permutation(np.resize(levels, k // 32))).repeat(32)
    a = np.empty((k // 512, 16))
    for p in range(k // 512):
        a[p, :8] = np.random.permutation(np.resize(levels, 8))
        for g in range(8):
            far = levels[np.abs(levels - a[p, g]) >= 10]
            a[p, g + 8] = far[np.random.randint(len(far))]
    return np.exp2(a.ravel()).repeat(32)


def f64(x):
    return np.asarray(x).astype(np.float64)


def striped(idx):
    return np.tile(np.asarray(idx).reshape(-1, 16).T, (8, 1)).astype(np.uint16)


def unstriped(offs):
    return offs[:16].T.reshape(-1).astype(np.int64)


E2M1 = np.array([0.0, 0.5, 1.0, 1.5, 2.0, 3.0, 4.0, 6.0, -0.0, -0.5, -1.0, -1.5, -2.0, -3.0, -4.0, -6.0])


def pack_weight(w, fmt):
    k, n = w.shape
    w = f64(np.asarray(w, np.float32).astype(ml_dtypes.bfloat16)).reshape(k // 32, 32, n)
    amax = np.abs(w).max(1)
    if fmt == "e4m3":
        byte = np.frexp(amax)[1] - 1 + 127 - 7
    else:
        mant, ex = np.frexp(amax / 6.0)
        byte = np.where(mant > 0.5, ex, ex - 1) + 127
    byte = np.clip(np.where(amax > 0, byte, 1), 1, 254)
    scaled = (w * np.exp2(127.0 - byte)[:, None, :]).reshape(k, n).astype(np.float32)
    by_word = np.ascontiguousarray(scaled.reshape(k // 512, 128, 4, n).transpose(0, 1, 3, 2))
    if fmt == "e4m3":
        words = by_word.astype(ml_dtypes.float8_e4m3fn).view(np.uint8)
    else:
        c = by_word.astype(ml_dtypes.float4_e2m1fn).view(np.uint8) & 0xF
        words = (c[..., 0::2] | (c[..., 1::2] << 4)).reshape(k // 512, 128, 2 * n)
    return np.ascontiguousarray(words), np.ascontiguousarray(byte.astype(np.uint8).reshape(k // 512, 16, n))


def unpack_weight(words, scales, fmt):
    g, _, n = scales.shape
    words = np.ascontiguousarray(words).reshape(g, 128, n, -1)
    if fmt == "e4m3":
        vals = words.view(ml_dtypes.float8_e4m3fn).astype(np.float64)
    else:
        nib = np.empty((g, 128, n, 4), np.uint8)
        nib[..., 0::2] = words & 0xF
        nib[..., 1::2] = words >> 4
        vals = E2M1[nib]
    vals = vals * np.repeat(np.exp2(scales.astype(np.float64) - 127.0), 8, axis=1)[..., None]
    return vals.transpose(0, 1, 3, 2).reshape(g * 512, n)


def sigmoid(v):
    return 1.0 / (1.0 + np.exp(-v))


D, E, T, I, Q, G = 512, 512, 2048, 512, 128, 64


def setup_inputs():
    n = np.random.standard_normal
    idx = np.random.permutation(T)[:I]
    fd = mx_kscale(D)
    fe = mx_kscale(E)
    keysp = pack_weight(n((D, T)) / fd[:, None], "e4m3")
    valsp = pack_weight(n((E, T)) / fe[:, None], "e4m3")
    return {
        "query": (n((D, Q)) * 0.6 / np.sqrt(D) * fd[:, None]).astype(np.float32),
        "keys_words": keysp[0],
        "keys_scales": keysp[1],
        "gout": (n((E, Q)) * 1 / np.sqrt(E) * fe[:, None]).astype(np.float32),
        "vals_words": valsp[0],
        "vals_scales": valsp[1],
        "size": (np.random.uniform(0.5, 2.0, (1, I))).astype(np.float32),
        "old": (0.5 * n((Q, T))).astype(np.float32),
        "offs": striped(idx),
    }


def reference(query, keys_words, keys_scales, gout, vals_words, vals_scales, size, old, offs):
    idx = unstriped(offs)
    keysu = unpack_weight(keys_words, keys_scales, "e4m3")
    valsu = unpack_weight(vals_words, vals_scales, "e4m3")
    queryq = mxq(f64(query), 0, "e4m3")
    keysidxg = keysu[:, idx]
    a = queryq.T @ keysidxg
    s = a.reshape(Q, G, I // G).mean(axis=2)
    p = np.exp(s - np.max(s, axis=1, keepdims=True))
    z = np.sum(p, axis=1, keepdims=True)
    r = p / z
    rr = np.repeat(r, I // G, axis=1)
    goutq = mxq(f64(gout), 0, "e4m3")
    valsidxg = valsu[:, idx]
    c0 = goutq.T @ valsidxg
    drr = c0 * f64(size) * sigmoid(a)
    dr = drr.reshape(Q, G, I // G).sum(axis=2)
    dz = np.sum(dr * p / np.square(z) * (-1.0), axis=1, keepdims=True)
    dp = dr / z + dz
    ds = dp * p
    e1 = ds / 8.0
    r1 = np.repeat(e1, I // G, axis=1)
    da = c0 * f64(size) * rr * sigmoid(a) * (1.0 - sigmoid(a)) + r1
    gs = da * 64.0
    gf = np.zeros((Q, T))
    gf[:, idx] = gs
    y = f64(old) + gf
    return y

@@ -1,0 +1,169 @@
+from contextlib import ExitStack
+
+import concourse.mybir as mybir
+from concourse.masks import make_identity
+
+D, E, T, I, Q, G = 512, 512, 2048, 512, 128, 64
+FLOPS = 2 * Q * I * (D + E)
+
+F32 = mybir.dt.float32
+BF16 = mybir.dt.bfloat16
+I32 = mybir.dt.int32
+U32 = mybir.dt.uint32
+U16 = mybir.dt.uint16
+U8 = mybir.dt.uint8
+FP8X4 = mybir.dt.float8_e4m3fn_x4
+ALU = mybir.AluOpType
+ACT = mybir.ActivationFunctionType
+AX = mybir.AxisListType
+
+P = 128
+PACK = 4
+SPAN = I // G
+HALF = I // 2
+STORE_WIDTHS = (256, 512, 512, 512, 256)
+
+
+def tile_attend_bspanread_s_kernel(tc, query, keys_words, keys_scales, gout, vals_words, vals_scales, size, old, offs, out):
+    nc = tc.nc
+    with ExitStack() as ctx:
+        keep = ctx.enter_context(tc.tile_pool(name="keep", bufs=1))
+        psum = ctx.enter_context(tc.psum_pool(name="psum", bufs=1))
+
+        offsets = keep.tile([P, I // 16], U16, name="offsets")
+        nc.sync.dma_start(offsets[:], offs)
+
+        warm = keep.tile([P, 2], F32, name="warm")
+        nc.vector.memset(warm[:, 0:1], 0.0)
+        nc.scalar.activation(warm[:, 1:2], warm[:, 0:1], ACT.Exp)
+
+        k_bytes = keep.tile([P, T], U8, name="k_bytes", align_bytes=64)
+        v_bytes = keep.tile([P, T], U8, name="v_bytes", align_bytes=64)
+        for tile, rows, first in ((k_bytes, keys_scales, 0), (v_bytes, vals_scales, 64)):
+            nc.sync.dma_start(tile[first : first + 32, :].bitcast(I32), rows[0].bitcast(I32).unsqueeze(1).to_broadcast([16, 2, T // 4]))
+        for tile, parts in ((k_bytes, ((32, 64), (64, 128))), (v_bytes, ((0, 64), (96, 128)))):
+            for lo, hi in parts:
+                nc.vector.memset(tile[lo:hi, :].bitcast(I32), 0)
+
+        size_col = keep.tile([P, PACK], F32, name="size_col")
+        nc.sync.dma_start(size_col[:], size[0].rearrange("(p c) -> p c", c=PACK))
+        q_raw = keep.tile([P, PACK, Q], F32, name="q_raw", tag="pool_b", align_bytes=64)
+        nc.sync.dma_start(q_raw[:], query.rearrange("(p j) q -> p j q", j=PACK))
+        k_words = keep.tile([P, T], U32, name="k_words", tag="pool_a", align_bytes=64)
+        nc.sync.dma_start(k_words[:].bitcast(I32), keys_words[0].rearrange("p n t -> p (n t)").bitcast(I32))
+        g_raw = keep.tile([P, PACK, Q], F32, name="g_raw")
+        nc.sync.dma_start(g_raw[:], gout.rearrange("(p j) q -> p j q", j=PACK))
+
+        ident = keep.tile([P, P], F32, name="ident")
+        make_identity(nc, ident[:])
+
+        window = keep.tile([P, T], F32, name="window")
+        for at in range(0, T, 256):
+            nc.vector.memset(window[:, at : at + 256], 0.0)
+
+        def quantise(raw, name):
+            grouped = keep.tile([P, Q, PACK], BF16, name=name + "_grouped", align_bytes=64)
+            nc.scalar.copy(grouped[:], raw[:].rearrange("p j q -> p q j"))
+            codes = keep.tile([P, Q], U32, name=name + "_codes", align_bytes=64)
+            scales = keep.tile([P, Q], U8, name=name + "_scales", align_bytes=64)
+            nc.vector.quantize_mx(out=codes[:].bitcast(FP8X4), scales=scales[:], in_=grouped[:].rearrange("p q j -> p (q j)"))
+            return codes, scales
+
+        def scale_plane(queue, pool_bytes, first, name):
+            listed = keep.tile([P, I], U8, name=name + "_listed", align_bytes=64)
+            nc.vector.tensor_copy(listed[:], pool_bytes[:].indirect(offsets[:]))
+            plane = keep.tile([P, I], U8, name=name + "_plane", align_bytes=64)
+            for quadrant in range(4):
+                at = first + 8 * quadrant
+                queue.dma_start(plane[32 * quadrant : 32 * quadrant + 4, :].bitcast(I32), listed[at : at + 8 : 2, :].bitcast(I32))
+            return plane
+
+        k_scale = scale_plane(nc.scalar, k_bytes, 0, "k")
+        q_codes, q_scales = quantise(q_raw, "q")
+        v_words = keep.tile([P, T], U32, name="v_words", tag="pool_b", align_bytes=64)
+        nc.sync.dma_start(v_words[:].bitcast(I32), vals_words[0].rearrange("p n t -> p (n t)").bitcast(I32))
+        v_scale = scale_plane(nc.sync, v_bytes, 64, "v")
+
+        size_bank = psum.tile([P, PACK, P], F32, name="size_bank")
+        for c in range(PACK):
+            nc.tensor.transpose(size_bank[:, c, :], size_col[:, c : c + 1].to_broadcast([P, P]), ident[:])
+        size_row = keep.tile([P, P, PACK], F32, name="size_row")
+        nc.scalar.copy(size_row[:], size_bank[:].rearrange("p c n -> p n c"))
+
+        th = keep.tile([P, I], F32, name="th")
+        span_sum = keep.tile([P, G], F32, name="span_sum")
+        scores = []
+        for h in range(2):
+            cols = slice(h * HALF, (h + 1) * HALF)
+            k_codes = keep.tile([P, HALF], U32, name="k_codes%d" % h, align_bytes=64)
+            nc.vector.tensor_copy(k_codes[:], k_words[:].indirect(offsets[:, h * (HALF // 16) : (h + 1) * (HALF // 16)]))
+            a = psum.tile([P, HALF], F32, name="a%d" % h)
+            nc.tensor.matmul_mx(out=a[:], lhsT=q_codes[:].bitcast(FP8X4), lhsT_scale=q_scales[:], rhs=k_codes[:].bitcast(FP8X4), rhs_scale=k_scale[:, cols], start=True, stop=True)
+            scores.append(a)
+
+        old_rows = keep.tile([P, T], F32, name="old_rows", tag="pool_a", align_bytes=64)
+        nc.sync.dma_start(old_rows[:], old)
+
+        def span_sums(h):
+            nc.vector.tensor_reduce(span_sum[:, h * (G // 2) : (h + 1) * (G // 2)], scores[h][:].rearrange("p (g j) -> p g j", j=SPAN), AX.X, ALU.add)
+
+        def tanh_half(h):
+            nc.scalar.activation(th[:, h * HALF : (h + 1) * HALF], scores[h][:], ACT.Tanh, scale=0.5)
+
+        tanh_half(0)
+        span_sums(0)
+        span_sums(1)
+        tanh_half(1)
+
+        neg_s = keep.tile([P, G], F32, name="neg_s")
+        neg_max = keep.tile([P, 1], F32, name="neg_max")
+        nc.vector.tensor_scalar(neg_s[:], span_sum[:], -1.0 / SPAN, None, ALU.mult, ALU.min, accum_out=neg_max[:])
+        p = keep.tile([P, G], F32, name="p")
+        z = keep.tile([P, 1], F32, name="z")
+        nc.scalar.activation(p[:], neg_s[:], ACT.Exp, bias=neg_max[:], scale=-1.0, accum_out=z[:])
+
+        g_codes, g_scales = quantise(g_raw, "g")
+
+        def spread(small):
+            return small[:].unsqueeze(2).to_broadcast([P, G, SPAN])
+
+        def by_span(wide):
+            return wide[:].rearrange("p (g j) -> p g j", j=SPAN)
+
+        size_p = keep.tile([P, I], F32, name="size_p")
+        nc.vector.tensor_tensor(by_span(size_p), size_row[:].rearrange("p (g a) c -> p g (a c)", g=G), spread(p), ALU.mult)
+        inv_z = keep.tile([P, 1], F32, name="inv_z")
+        nc.vector.reciprocal(inv_z[:], z[:])
+
+        v_codes = keep.tile([P, I], U32, name="v_codes", align_bytes=64)
+        nc.vector.tensor_copy(v_codes[:], v_words[:].indirect(offsets[:]))
+        c0 = psum.tile([P, I], F32, name="c0")
+        nc.tensor.matmul_mx(out=c0[:], lhsT=g_codes[:].bitcast(FP8X4), lhsT_scale=g_scales[:], rhs=v_codes[:].bitcast(FP8X4), rhs_scale=v_scale[:], start=True, stop=True)
+
+        weight = keep.tile([P, I], F32, name="weight")
+        nc.vector.scalar_tensor_tensor(weight[:], th[:], 1.0, size_p[:], ALU.add, ALU.mult)
+        r = keep.tile([P, G], F32, name="r")
+        nc.scalar.activation(r[:], p[:], ACT.Copy, scale=inv_z[:])
+        rest = keep.tile([P, I], F32, name="rest")
+        nc.scalar.activation(rest[:], th[:], ACT.Copy, bias=16.0, scale=-16.0)
+
+        u = keep.tile([P, I], F32, name="u")
+        u_total = keep.tile([P, 1], F32, name="u_total")
+        nc.vector.scalar_tensor_tensor(u[:], c0[:], inv_z[:], weight[:], ALU.mult, ALU.mult, accum_out=u_total[:])
+        u_span = keep.tile([P, G], F32, name="u_span")
+        nc.vector.tensor_reduce(u_span[:], by_span(u), AX.X, ALU.add)
+        neg_e = keep.tile([P, G], F32, name="neg_e")
+        nc.vector.scalar_tensor_tensor(neg_e[:], r[:], u_total[:], u_span[:], ALU.mult, ALU.subtract)
+        own = keep.tile([P, I], F32, name="own")
+        nc.vector.tensor_tensor(own[:], u[:], rest[:], ALU.mult)
+        shared = keep.tile([P, I], F32, name="shared")
+        nc.scalar.activation(by_span(shared), spread(neg_e), ACT.Copy, scale=-4.0)
+        nc.vector.tensor_tensor(window[:].indirect(offsets[:]), own[:], shared[:], ALU.add)
+
+        at = 0
+        for n, width in enumerate(STORE_WIDTHS):
+            cols = slice(at, at + width)
+            total = keep.tile([P, width], F32, name="total%d" % n)
+            nc.vector.tensor_tensor(total[:], window[:, cols], old_rows[:, cols], ALU.add)
+            nc.sync.dma_start(out[:, cols], total[:])
+            at = at + width

@@ -30,135 +30,143 @@ def tile_attend_bspanread_s_kernel(tc, query, keys_words, keys_scales, gout, val
         keep = ctx.enter_context(tc.tile_pool(name="keep", bufs=1))
         psum = ctx.enter_context(tc.psum_pool(name="psum", bufs=1))
 
+        def slots(h):
+            return slice(h * HALF, (h + 1) * HALF)
+
+        def spans(h):
+            return slice(h * (G // 2), (h + 1) * (G // 2))
+
+        def by_span(ap):
+            return ap.rearrange("p (g j) -> p g j", j=SPAN)
+
+        def spread(ap):
+            return ap.unsqueeze(2).to_broadcast([P, ap.shape[1], SPAN])
+
         offsets = keep.tile([P, I // 16], U16, name="offsets")
         nc.sync.dma_start(offsets[:], offs)
+
+        def listed(h):
+            return offsets[:, h * (HALF // 16) : (h + 1) * (HALF // 16)]
+
+        size_col = keep.tile([P, PACK], F32, name="size_col", tag="size_col", align_bytes=64)
+        nc.sync.dma_start(size_col[:], size[0].rearrange("(p c) -> p c", c=PACK))
+
+        k_bytes = keep.tile([P, T], U8, name="k_bytes", tag="keys_then_old", align_bytes=64)
+        nc.vector.memset(k_bytes[:].bitcast(I32), 0)
+        for quadrant in range(4):
+            nc.scalar.dma_start(k_bytes[32 * quadrant : 32 * quadrant + 4, :].bitcast(I32), keys_scales[0, 4 * quadrant : 4 * quadrant + 4, :].bitcast(I32))
+
+        v_bytes = keep.tile([P, T], U8, name="v_bytes", tag="vals", align_bytes=64)
+        nc.sync.dma_start(v_bytes[64:96, :].bitcast(I32), vals_scales[0].bitcast(I32).unsqueeze(1).to_broadcast([16, 2, T // 4]))
+        nc.vector.memset(v_bytes[0:64, :].bitcast(I32), 0)
+        nc.vector.memset(v_bytes[96:128, :].bitcast(I32), 0)
 
         warm = keep.tile([P, 2], F32, name="warm")
         nc.vector.memset(warm[:, 0:1], 0.0)
         nc.scalar.activation(warm[:, 1:2], warm[:, 0:1], ACT.Exp)
 
-        k_bytes = keep.tile([P, T], U8, name="k_bytes", align_bytes=64)
-        v_bytes = keep.tile([P, T], U8, name="v_bytes", align_bytes=64)
-        for tile, rows, first in ((k_bytes, keys_scales, 0), (v_bytes, vals_scales, 64)):
-            nc.sync.dma_start(tile[first : first + 32, :].bitcast(I32), rows[0].bitcast(I32).unsqueeze(1).to_broadcast([16, 2, T // 4]))
-        for tile, parts in ((k_bytes, ((32, 64), (64, 128))), (v_bytes, ((0, 64), (96, 128)))):
-            for lo, hi in parts:
-                nc.vector.memset(tile[lo:hi, :].bitcast(I32), 0)
+        def load_rows(rows, name):
+            raw = keep.tile([P, PACK, Q], F32, name=name)
+            nc.sync.dma_start(raw[:], rows.rearrange("(p j) q -> p j q", j=PACK))
+            return raw
 
-        size_col = keep.tile([P, PACK], F32, name="size_col")
-        nc.sync.dma_start(size_col[:], size[0].rearrange("(p c) -> p c", c=PACK))
-        q_raw = keep.tile([P, PACK, Q], F32, name="q_raw", tag="pool_b", align_bytes=64)
-        nc.sync.dma_start(q_raw[:], query.rearrange("(p j) q -> p j q", j=PACK))
-        k_words = keep.tile([P, T], U32, name="k_words", tag="pool_a", align_bytes=64)
-        nc.sync.dma_start(k_words[:].bitcast(I32), keys_words[0].rearrange("p n t -> p (n t)").bitcast(I32))
-        g_raw = keep.tile([P, PACK, Q], F32, name="g_raw")
-        nc.sync.dma_start(g_raw[:], gout.rearrange("(p j) q -> p j q", j=PACK))
+        def load_words(words, name, tag):
+            tile = keep.tile([P, T], U32, name=name, tag=tag, align_bytes=64)
+            nc.sync.dma_start(tile[:].bitcast(I32), words[0].rearrange("p n t -> p (n t)").bitcast(I32))
+            return tile
 
-        ident = keep.tile([P, P], F32, name="ident")
+        q_raw = load_rows(query, "q_raw")
+        k_words = load_words(keys_words, "k_words", "k_words")
+        g_raw = load_rows(gout, "g_raw")
+
+        ident = keep.tile([P, P], F32, name="ident", tag="ident", align_bytes=64)
         make_identity(nc, ident[:])
 
-        window = keep.tile([P, T], F32, name="window")
-        for at in range(0, T, 256):
-            nc.vector.memset(window[:, at : at + 256], 0.0)
-
-        def quantise(raw, name):
-            grouped = keep.tile([P, Q, PACK], BF16, name=name + "_grouped", align_bytes=64)
+        def quantise(raw, name, tag):
+            grouped = keep.tile([P, Q, PACK], BF16, name=name + "_grouped", tag=tag, align_bytes=64)
             nc.scalar.copy(grouped[:], raw[:].rearrange("p j q -> p q j"))
             codes = keep.tile([P, Q], U32, name=name + "_codes", align_bytes=64)
             scales = keep.tile([P, Q], U8, name=name + "_scales", align_bytes=64)
             nc.vector.quantize_mx(out=codes[:].bitcast(FP8X4), scales=scales[:], in_=grouped[:].rearrange("p q j -> p (q j)"))
             return codes, scales
 
-        def scale_plane(queue, pool_bytes, first, name):
-            listed = keep.tile([P, I], U8, name=name + "_listed", align_bytes=64)
-            nc.vector.tensor_copy(listed[:], pool_bytes[:].indirect(offsets[:]))
-            plane = keep.tile([P, I], U8, name=name + "_plane", align_bytes=64)
-            for quadrant in range(4):
-                at = first + 8 * quadrant
-                queue.dma_start(plane[32 * quadrant : 32 * quadrant + 4, :].bitcast(I32), listed[at : at + 8 : 2, :].bitcast(I32))
-            return plane
+        v_rows = keep.tile([P, I], U8, name="v_rows", align_bytes=64)
+        nc.vector.tensor_copy(v_rows[:], v_bytes[:].indirect(offsets[:]))
+        v_words = load_words(vals_words, "v_words", "vals")
+        v_scale = keep.tile([P, I], U8, name="v_scale", align_bytes=64)
+        for quadrant in range(4):
+            at = 64 + 8 * quadrant
+            nc.sync.dma_start(v_scale[32 * quadrant : 32 * quadrant + 4, :].bitcast(I32), v_rows[at : at + 8 : 2, :].bitcast(I32))
 
-        k_scale = scale_plane(nc.scalar, k_bytes, 0, "k")
-        q_codes, q_scales = quantise(q_raw, "q")
-        v_words = keep.tile([P, T], U32, name="v_words", tag="pool_b", align_bytes=64)
-        nc.sync.dma_start(v_words[:].bitcast(I32), vals_words[0].rearrange("p n t -> p (n t)").bitcast(I32))
-        v_scale = scale_plane(nc.sync, v_bytes, 64, "v")
+        k_scale = keep.tile([P, I], U8, name="k_scale", align_bytes=64)
+        nc.vector.tensor_copy(k_scale[:], k_bytes[:].indirect(offsets[:]))
+        old_rows = keep.tile([P, T], F32, name="old_rows", tag="keys_then_old", align_bytes=64)
+        nc.sync.dma_start(old_rows[:], old)
+        q_codes, q_scales = quantise(q_raw, "q", "q_grouped")
 
         size_bank = psum.tile([P, PACK, P], F32, name="size_bank")
         for c in range(PACK):
             nc.tensor.transpose(size_bank[:, c, :], size_col[:, c : c + 1].to_broadcast([P, P]), ident[:])
-        size_row = keep.tile([P, P, PACK], F32, name="size_row")
-        nc.scalar.copy(size_row[:], size_bank[:].rearrange("p c n -> p n c"))
+        size_row = keep.tile([P, I], F32, name="size_row", tag="size_row", align_bytes=64)
+        nc.scalar.copy(size_row[:].rearrange("p (n c) -> p n c", c=PACK), size_bank[:].rearrange("p c n -> p n c"))
+
+        def product(words, picked, scale, codes, scales, h, name):
+            nc.vector.tensor_copy(picked[:, slots(h)], words[:].indirect(listed(h)))
+            bank = psum.tile([P, HALF], F32, name="%s%d" % (name, h))
+            nc.tensor.matmul_mx(out=bank[:], lhsT=codes[:].bitcast(FP8X4), lhsT_scale=scales[:], rhs=picked[:, slots(h)].bitcast(FP8X4), rhs_scale=scale[:, slots(h)], start=True, stop=True)
+            return bank
+
+        k_picked = keep.tile([P, I], U32, name="k_picked", tag="size_col", align_bytes=64)
+        a = [product(k_words, k_picked, k_scale, q_codes, q_scales, h, "a") for h in range(2)]
 
         th = keep.tile([P, I], F32, name="th")
         span_sum = keep.tile([P, G], F32, name="span_sum")
-        scores = []
+        nc.scalar.activation(th[:, slots(0)], a[0][:], ACT.Tanh, scale=0.5)
         for h in range(2):
-            cols = slice(h * HALF, (h + 1) * HALF)
-            k_codes = keep.tile([P, HALF], U32, name="k_codes%d" % h, align_bytes=64)
-            nc.vector.tensor_copy(k_codes[:], k_words[:].indirect(offsets[:, h * (HALF // 16) : (h + 1) * (HALF // 16)]))
-            a = psum.tile([P, HALF], F32, name="a%d" % h)
-            nc.tensor.matmul_mx(out=a[:], lhsT=q_codes[:].bitcast(FP8X4), lhsT_scale=q_scales[:], rhs=k_codes[:].bitcast(FP8X4), rhs_scale=k_scale[:, cols], start=True, stop=True)
-            scores.append(a)
+            nc.vector.tensor_reduce(span_sum[:, spans(h)], by_span(a[h][:]), AX.X, ALU.add)
+        nc.scalar.activation(th[:, slots(1)], a[1][:], ACT.Tanh, scale=0.5)
 
-        old_rows = keep.tile([P, T], F32, name="old_rows", tag="pool_a", align_bytes=64)
-        nc.sync.dma_start(old_rows[:], old)
+        g_codes, g_scales = quantise(g_raw, "g", "ident")
 
-        def span_sums(h):
-            nc.vector.tensor_reduce(span_sum[:, h * (G // 2) : (h + 1) * (G // 2)], scores[h][:].rearrange("p (g j) -> p g j", j=SPAN), AX.X, ALU.add)
-
-        def tanh_half(h):
-            nc.scalar.activation(th[:, h * HALF : (h + 1) * HALF], scores[h][:], ACT.Tanh, scale=0.5)
-
-        tanh_half(0)
-        span_sums(0)
-        span_sums(1)
-        tanh_half(1)
-
+        weight = keep.tile([P, I], F32, name="weight")
+        nc.vector.scalar_tensor_tensor(weight[:, slots(0)], th[:, slots(0)], 1.0, size_row[:, slots(0)], ALU.add, ALU.mult)
         neg_s = keep.tile([P, G], F32, name="neg_s")
         neg_max = keep.tile([P, 1], F32, name="neg_max")
         nc.vector.tensor_scalar(neg_s[:], span_sum[:], -1.0 / SPAN, None, ALU.mult, ALU.min, accum_out=neg_max[:])
+        nc.vector.scalar_tensor_tensor(weight[:, slots(1)], th[:, slots(1)], 1.0, size_row[:, slots(1)], ALU.add, ALU.mult)
         p = keep.tile([P, G], F32, name="p")
         z = keep.tile([P, 1], F32, name="z")
         nc.scalar.activation(p[:], neg_s[:], ACT.Exp, bias=neg_max[:], scale=-1.0, accum_out=z[:])
+        rest = keep.tile([P, I], F32, name="rest")
+        nc.scalar.activation(rest[:], th[:], ACT.Copy, bias=4.0, scale=-4.0)
 
-        g_codes, g_scales = quantise(g_raw, "g")
+        v_picked = keep.tile([P, I], U32, name="v_picked", tag="size_row", align_bytes=64)
+        c0 = [product(v_words, v_picked, v_scale, g_codes, g_scales, h, "c") for h in range(2)]
 
-        def spread(small):
-            return small[:].unsqueeze(2).to_broadcast([P, G, SPAN])
-
-        def by_span(wide):
-            return wide[:].rearrange("p (g j) -> p g j", j=SPAN)
-
-        size_p = keep.tile([P, I], F32, name="size_p")
-        nc.vector.tensor_tensor(by_span(size_p), size_row[:].rearrange("p (g a) c -> p g (a c)", g=G), spread(p), ALU.mult)
         inv_z = keep.tile([P, 1], F32, name="inv_z")
         nc.vector.reciprocal(inv_z[:], z[:])
-
-        v_codes = keep.tile([P, I], U32, name="v_codes", align_bytes=64)
-        nc.vector.tensor_copy(v_codes[:], v_words[:].indirect(offsets[:]))
-        c0 = psum.tile([P, I], F32, name="c0")
-        nc.tensor.matmul_mx(out=c0[:], lhsT=g_codes[:].bitcast(FP8X4), lhsT_scale=g_scales[:], rhs=v_codes[:].bitcast(FP8X4), rhs_scale=v_scale[:], start=True, stop=True)
-
-        weight = keep.tile([P, I], F32, name="weight")
-        nc.vector.scalar_tensor_tensor(weight[:], th[:], 1.0, size_p[:], ALU.add, ALU.mult)
-        r = keep.tile([P, G], F32, name="r")
-        nc.scalar.activation(r[:], p[:], ACT.Copy, scale=inv_z[:])
-        rest = keep.tile([P, I], F32, name="rest")
-        nc.scalar.activation(rest[:], th[:], ACT.Copy, bias=16.0, scale=-16.0)
+        share = keep.tile([P, I], F32, name="share")
+        nc.scalar.activation(by_span(share[:]), spread(p[:]), ACT.Copy, scale=inv_z[:])
 
         u = keep.tile([P, I], F32, name="u")
-        u_total = keep.tile([P, 1], F32, name="u_total")
-        nc.vector.scalar_tensor_tensor(u[:], c0[:], inv_z[:], weight[:], ALU.mult, ALU.mult, accum_out=u_total[:])
         u_span = keep.tile([P, G], F32, name="u_span")
-        nc.vector.tensor_reduce(u_span[:], by_span(u), AX.X, ALU.add)
-        neg_e = keep.tile([P, G], F32, name="neg_e")
-        nc.vector.scalar_tensor_tensor(neg_e[:], r[:], u_total[:], u_span[:], ALU.mult, ALU.subtract)
         own = keep.tile([P, I], F32, name="own")
-        nc.vector.tensor_tensor(own[:], u[:], rest[:], ALU.mult)
-        shared = keep.tile([P, I], F32, name="shared")
-        nc.scalar.activation(by_span(shared), spread(neg_e), ACT.Copy, scale=-4.0)
-        nc.vector.tensor_tensor(window[:].indirect(offsets[:]), own[:], shared[:], ALU.add)
+        for h in range(2):
+            nc.vector.scalar_tensor_tensor(u[:, slots(h)], c0[h][:], 4.0, weight[:, slots(h)], ALU.mult, ALU.mult)
+        for h in range(2):
+            nc.vector.tensor_reduce(u_span[:, spans(h)], by_span(u[:, slots(h)]), AX.X, ALU.add)
+        nc.vector.tensor_tensor(own[:, slots(0)], u[:, slots(0)], rest[:, slots(0)], ALU.mult)
+        weighed = keep.tile([P, G], F32, name="weighed")
+        mean = keep.tile([P, 1], F32, name="mean")
+        nc.vector.scalar_tensor_tensor(weighed[:], u_span[:], inv_z[:], p[:], ALU.mult, ALU.mult, accum_out=mean[:])
+        nc.vector.tensor_tensor(own[:, slots(1)], u[:, slots(1)], rest[:, slots(1)], ALU.mult)
+        grad = keep.tile([P, I], F32, name="grad")
+        for h in range(2):
+            nc.vector.scalar_tensor_tensor(by_span(grad[:, slots(h)]), spread(u_span[:, spans(h)]), mean[:], by_span(own[:, slots(h)]), ALU.subtract, ALU.add)
+        window = keep.tile([P, T], F32, name="window")
+        for at in range(0, T, 256):
+            nc.vector.memset(window[:, at : at + 256], 0.0)
+        nc.vector.tensor_tensor(window[:].indirect(offsets[:]), grad[:], share[:], ALU.mult)
 
         at = 0
         for n, width in enumerate(STORE_WIDTHS):

@@ -48,16 +48,23 @@ def tile_attend_bspanread_s_kernel(tc, query, keys_words, keys_scales, gout, val
         def listed(h):
             return offsets[:, h * (HALF // 16) : (h + 1) * (HALF // 16)]
 
-        size_col = keep.tile([P, PACK], F32, name="size_col", tag="size_col", align_bytes=64)
-        nc.sync.dma_start(size_col[:], size[0].rearrange("(p c) -> p c", c=PACK))
+        def load_rows(rows, name):
+            raw = keep.tile([P, PACK, Q], F32, name=name)
+            nc.sync.dma_start(raw[:], rows.rearrange("(p j) q -> p j q", j=PACK))
+            return raw
+
+        def load_words(words, name):
+            tile = keep.tile([P, T], U32, name=name, tag=name, align_bytes=64)
+            nc.sync.dma_start(tile[:].bitcast(I32), words[0].rearrange("p n t -> p (n t)").bitcast(I32))
+            return tile
 
         k_bytes = keep.tile([P, T], U8, name="k_bytes", tag="keys_then_old", align_bytes=64)
         nc.vector.memset(k_bytes[:].bitcast(I32), 0)
-        for quadrant in range(4):
-            nc.scalar.dma_start(k_bytes[32 * quadrant : 32 * quadrant + 4, :].bitcast(I32), keys_scales[0, 4 * quadrant : 4 * quadrant + 4, :].bitcast(I32))
-
-        v_bytes = keep.tile([P, T], U8, name="v_bytes", tag="vals", align_bytes=64)
+        v_bytes = keep.tile([P, T], U8, name="v_bytes", align_bytes=64)
         nc.sync.dma_start(v_bytes[64:96, :].bitcast(I32), vals_scales[0].bitcast(I32).unsqueeze(1).to_broadcast([16, 2, T // 4]))
+        q_raw = load_rows(query, "q_raw")
+        for quadrant in range(4):
+            nc.sync.dma_start(k_bytes[32 * quadrant : 32 * quadrant + 4, :].bitcast(I32), keys_scales[0, 4 * quadrant : 4 * quadrant + 4, :].bitcast(I32))
         nc.vector.memset(v_bytes[0:64, :].bitcast(I32), 0)
         nc.vector.memset(v_bytes[96:128, :].bitcast(I32), 0)
 
@@ -65,25 +72,17 @@ def tile_attend_bspanread_s_kernel(tc, query, keys_words, keys_scales, gout, val
         nc.vector.memset(warm[:, 0:1], 0.0)
         nc.scalar.activation(warm[:, 1:2], warm[:, 0:1], ACT.Exp)
 
-        def load_rows(rows, name):
-            raw = keep.tile([P, PACK, Q], F32, name=name)
-            nc.sync.dma_start(raw[:], rows.rearrange("(p j) q -> p j q", j=PACK))
-            return raw
-
-        def load_words(words, name, tag):
-            tile = keep.tile([P, T], U32, name=name, tag=tag, align_bytes=64)
-            nc.sync.dma_start(tile[:].bitcast(I32), words[0].rearrange("p n t -> p (n t)").bitcast(I32))
-            return tile
-
-        q_raw = load_rows(query, "q_raw")
-        k_words = load_words(keys_words, "k_words", "k_words")
+        k_words = load_words(keys_words, "k_words")
+        size_col = keep.tile([P, 2, 8], F32, name="size_col")
+        nc.sync.dma_start(size_col[:, :, 0:2], size[0].rearrange("(h p e) -> p h e", h=2, e=2))
         g_raw = load_rows(gout, "g_raw")
+        v_words = load_words(vals_words, "v_words")
 
-        ident = keep.tile([P, P], F32, name="ident", tag="ident", align_bytes=64)
+        ident = keep.tile([P, P], F32, name="ident")
         make_identity(nc, ident[:])
 
-        def quantise(raw, name, tag):
-            grouped = keep.tile([P, Q, PACK], BF16, name=name + "_grouped", tag=tag, align_bytes=64)
+        def quantise(raw, name):
+            grouped = keep.tile([P, Q, PACK], BF16, name=name + "_grouped", align_bytes=64)
             nc.scalar.copy(grouped[:], raw[:].rearrange("p j q -> p q j"))
             codes = keep.tile([P, Q], U32, name=name + "_codes", align_bytes=64)
             scales = keep.tile([P, Q], U8, name=name + "_scales", align_bytes=64)
@@ -92,7 +91,6 @@ def tile_attend_bspanread_s_kernel(tc, query, keys_words, keys_scales, gout, val
 
         v_rows = keep.tile([P, I], U8, name="v_rows", align_bytes=64)
         nc.vector.tensor_copy(v_rows[:], v_bytes[:].indirect(offsets[:]))
-        v_words = load_words(vals_words, "v_words", "vals")
         v_scale = keep.tile([P, I], U8, name="v_scale", align_bytes=64)
         for quadrant in range(4):
             at = 64 + 8 * quadrant
@@ -102,48 +100,51 @@ def tile_attend_bspanread_s_kernel(tc, query, keys_words, keys_scales, gout, val
         nc.vector.tensor_copy(k_scale[:], k_bytes[:].indirect(offsets[:]))
         old_rows = keep.tile([P, T], F32, name="old_rows", tag="keys_then_old", align_bytes=64)
         nc.sync.dma_start(old_rows[:], old)
-        q_codes, q_scales = quantise(q_raw, "q", "q_grouped")
+        q_codes, q_scales = quantise(q_raw, "q")
 
-        size_bank = psum.tile([P, PACK, P], F32, name="size_bank")
-        for c in range(PACK):
-            nc.tensor.transpose(size_bank[:, c, :], size_col[:, c : c + 1].to_broadcast([P, P]), ident[:])
-        size_row = keep.tile([P, I], F32, name="size_row", tag="size_row", align_bytes=64)
-        nc.scalar.copy(size_row[:].rearrange("p (n c) -> p n c", c=PACK), size_bank[:].rearrange("p c n -> p n c"))
+        key_banks = [psum.tile([P, I], F32, name="key_bank%d" % h) for h in range(2)]
+        for h in range(2):
+            for e in range(2):
+                nc.tensor.transpose(key_banks[h][:, HALF + e * P : HALF + (e + 1) * P], size_col[:, h, e : e + 1].to_broadcast([P, P]), ident[:])
 
-        def product(words, picked, scale, codes, scales, h, name):
+        def product(bank, words, picked, scale, codes, scales, h):
             nc.vector.tensor_copy(picked[:, slots(h)], words[:].indirect(listed(h)))
-            bank = psum.tile([P, HALF], F32, name="%s%d" % (name, h))
-            nc.tensor.matmul_mx(out=bank[:], lhsT=codes[:].bitcast(FP8X4), lhsT_scale=scales[:], rhs=picked[:, slots(h)].bitcast(FP8X4), rhs_scale=scale[:, slots(h)], start=True, stop=True)
+            nc.tensor.matmul_mx(out=bank, lhsT=codes[:].bitcast(FP8X4), lhsT_scale=scales[:], rhs=picked[:, slots(h)].bitcast(FP8X4), rhs_scale=scale[:, slots(h)], start=True, stop=True)
             return bank
 
-        k_picked = keep.tile([P, I], U32, name="k_picked", tag="size_col", align_bytes=64)
-        a = [product(k_words, k_picked, k_scale, q_codes, q_scales, h, "a") for h in range(2)]
+        k_picked = keep.tile([P, I], U32, name="k_picked", align_bytes=64)
+        a = [product(key_banks[h][:, 0:HALF], k_words, k_picked, k_scale, q_codes, q_scales, h) for h in range(2)]
+
+        g_codes, g_scales = quantise(g_raw, "g")
 
         th = keep.tile([P, I], F32, name="th")
         span_sum = keep.tile([P, G], F32, name="span_sum")
-        nc.scalar.activation(th[:, slots(0)], a[0][:], ACT.Tanh, scale=0.5)
         for h in range(2):
-            nc.vector.tensor_reduce(span_sum[:, spans(h)], by_span(a[h][:]), AX.X, ALU.add)
-        nc.scalar.activation(th[:, slots(1)], a[1][:], ACT.Tanh, scale=0.5)
-
-        g_codes, g_scales = quantise(g_raw, "g", "ident")
+            nc.vector.tensor_reduce(span_sum[:, spans(h)], by_span(a[h]), AX.X, ALU.add)
+            nc.scalar.activation(th[:, slots(h)], a[h], ACT.Tanh, scale=0.5)
 
         weight = keep.tile([P, I], F32, name="weight")
-        nc.vector.scalar_tensor_tensor(weight[:, slots(0)], th[:, slots(0)], 1.0, size_row[:, slots(0)], ALU.add, ALU.mult)
+
+        def weigh(h):
+            size_half = key_banks[h][:, HALF:I].rearrange("p (e n) -> p n e", e=2)
+            nc.vector.scalar_tensor_tensor(weight[:, slots(h)].rearrange("p (n e) -> p n e", e=2), th[:, slots(h)].rearrange("p (n e) -> p n e", e=2), 1.0, size_half, ALU.add, ALU.mult)
+
+        weigh(0)
         neg_s = keep.tile([P, G], F32, name="neg_s")
         neg_max = keep.tile([P, 1], F32, name="neg_max")
         nc.vector.tensor_scalar(neg_s[:], span_sum[:], -1.0 / SPAN, None, ALU.mult, ALU.min, accum_out=neg_max[:])
-        nc.vector.scalar_tensor_tensor(weight[:, slots(1)], th[:, slots(1)], 1.0, size_row[:, slots(1)], ALU.add, ALU.mult)
+        weigh(1)
         p = keep.tile([P, G], F32, name="p")
         z = keep.tile([P, 1], F32, name="z")
         nc.scalar.activation(p[:], neg_s[:], ACT.Exp, bias=neg_max[:], scale=-1.0, accum_out=z[:])
         rest = keep.tile([P, I], F32, name="rest")
         nc.scalar.activation(rest[:], th[:], ACT.Copy, bias=4.0, scale=-4.0)
 
-        v_picked = keep.tile([P, I], U32, name="v_picked", tag="size_row", align_bytes=64)
-        c0 = [product(v_words, v_picked, v_scale, g_codes, g_scales, h, "c") for h in range(2)]
+        v_picked = keep.tile([P, I], U32, name="v_picked", align_bytes=64)
+        val_banks = [psum.tile([P, HALF], F32, name="val_bank%d" % h) for h in range(2)]
+        c0 = [product(val_banks[h][:], v_words, v_picked, v_scale, g_codes, g_scales, h) for h in range(2)]
 
-        inv_z = keep.tile([P, 1], F32, name="inv_z")
+        inv_z = keep.tile([P, 1], F32, name="inv_z", tag="v_words", align_bytes=64)
         nc.vector.reciprocal(inv_z[:], z[:])
         share = keep.tile([P, I], F32, name="share")
         nc.scalar.activation(by_span(share[:]), spread(p[:]), ACT.Copy, scale=inv_z[:])
@@ -152,7 +153,7 @@ def tile_attend_bspanread_s_kernel(tc, query, keys_words, keys_scales, gout, val
         u_span = keep.tile([P, G], F32, name="u_span")
         own = keep.tile([P, I], F32, name="own")
         for h in range(2):
-            nc.vector.scalar_tensor_tensor(u[:, slots(h)], c0[h][:], 4.0, weight[:, slots(h)], ALU.mult, ALU.mult)
+            nc.vector.scalar_tensor_tensor(u[:, slots(h)], c0[h], 4.0, weight[:, slots(h)], ALU.mult, ALU.mult)
         for h in range(2):
             nc.vector.tensor_reduce(u_span[:, spans(h)], by_span(u[:, slots(h)]), AX.X, ALU.add)
         nc.vector.tensor_tensor(own[:, slots(0)], u[:, slots(0)], rest[:, slots(0)], ALU.mult)
@@ -164,8 +165,8 @@ def tile_attend_bspanread_s_kernel(tc, query, keys_words, keys_scales, gout, val
         for h in range(2):
             nc.vector.scalar_tensor_tensor(by_span(grad[:, slots(h)]), spread(u_span[:, spans(h)]), mean[:], by_span(own[:, slots(h)]), ALU.subtract, ALU.add)
         window = keep.tile([P, T], F32, name="window")
-        for at in range(0, T, 256):
-            nc.vector.memset(window[:, at : at + 256], 0.0)
+        for at in range(0, T, 512):
+            nc.gpsimd.memset(window[:, at : at + 512], 0.0)
         nc.vector.tensor_tensor(window[:].indirect(offsets[:]), grad[:], share[:], ALU.mult)
 
         at = 0

@@ -119,21 +119,19 @@ def tile_attend_bspanread_s_kernel(tc, query, keys_words, keys_scales, gout, val
 
         th = keep.tile([P, I], F32, name="th")
         span_sum = keep.tile([P, G], F32, name="span_sum")
+        size_row = keep.tile([P, I], F32, name="size_row")
+        gate = keep.tile([P, I], F32, name="gate")
+        weight = keep.tile([P, I], F32, name="weight")
         for h in range(2):
             nc.vector.tensor_reduce(span_sum[:, spans(h)], by_span(a[h]), AX.X, ALU.add)
             nc.scalar.activation(th[:, slots(h)], a[h], ACT.Tanh, scale=0.5)
+            nc.scalar.copy(size_row[:, slots(h)].rearrange("p (n e) -> p n e", e=2), key_banks[h][:, HALF:I].rearrange("p (e n) -> p n e", e=2))
+            nc.scalar.activation(gate[:, slots(h)], th[:, slots(h)], ACT.Copy, bias=1.0, scale=1.0)
+            nc.gpsimd.tensor_tensor(weight[:, slots(h)], gate[:, slots(h)], size_row[:, slots(h)], ALU.mult)
 
-        weight = keep.tile([P, I], F32, name="weight")
-
-        def weigh(h):
-            size_half = key_banks[h][:, HALF:I].rearrange("p (e n) -> p n e", e=2)
-            nc.vector.scalar_tensor_tensor(weight[:, slots(h)].rearrange("p (n e) -> p n e", e=2), th[:, slots(h)].rearrange("p (n e) -> p n e", e=2), 1.0, size_half, ALU.add, ALU.mult)
-
-        weigh(0)
         neg_s = keep.tile([P, G], F32, name="neg_s")
         neg_max = keep.tile([P, 1], F32, name="neg_max")
         nc.vector.tensor_scalar(neg_s[:], span_sum[:], -1.0 / SPAN, None, ALU.mult, ALU.min, accum_out=neg_max[:])
-        weigh(1)
         p = keep.tile([P, G], F32, name="p")
         z = keep.tile([P, 1], F32, name="z")
         nc.scalar.activation(p[:], neg_s[:], ACT.Exp, bias=neg_max[:], scale=-1.0, accum_out=z[:])

@@ -21,6 +21,10 @@ P = 128
 PACK = 4
 SPAN = I // G
 HALF = I // 2
+QUADRANT = 32
+BLOCKS = 4
+PARKED = P - 16
+CLEAR_WIDTH = 512
 STORE_WIDTHS = (256, 512, 512, 512, 256)
 
 
@@ -42,11 +46,8 @@ def tile_attend_bspanread_s_kernel(tc, query, keys_words, keys_scales, gout, val
         def spread(ap):
             return ap.unsqueeze(2).to_broadcast([P, ap.shape[1], SPAN])
 
-        offsets = keep.tile([P, I // 16], U16, name="offsets")
-        nc.sync.dma_start(offsets[:], offs)
-
-        def listed(h):
-            return offsets[:, h * (HALF // 16) : (h + 1) * (HALF // 16)]
+        def plane_rows(plane, quadrant):
+            return plane[QUADRANT * quadrant : QUADRANT * quadrant + BLOCKS, :].bitcast(I32)
 
         def load_rows(rows, name):
             raw = keep.tile([P, PACK, Q], F32, name=name)
@@ -58,19 +59,20 @@ def tile_attend_bspanread_s_kernel(tc, query, keys_words, keys_scales, gout, val
             nc.sync.dma_start(tile[:].bitcast(I32), words[0].rearrange("p n t -> p (n t)").bitcast(I32))
             return tile
 
+        offsets = keep.tile([P, I // 16], U16, name="offsets")
+        nc.sync.dma_start(offsets[:], offs)
+
+        def listed(h):
+            return offsets[:, h * (HALF // 16) : (h + 1) * (HALF // 16)]
+
         k_bytes = keep.tile([P, T], U8, name="k_bytes", tag="keys_then_old", align_bytes=64)
         nc.vector.memset(k_bytes[:].bitcast(I32), 0)
         v_bytes = keep.tile([P, T], U8, name="v_bytes", align_bytes=64)
-        nc.sync.dma_start(v_bytes[64:96, :].bitcast(I32), vals_scales[0].bitcast(I32).unsqueeze(1).to_broadcast([16, 2, T // 4]))
+        nc.sync.dma_start(v_bytes[PARKED:P, :].bitcast(I32), vals_scales[0].bitcast(I32))
         q_raw = load_rows(query, "q_raw")
-        for quadrant in range(4):
-            nc.sync.dma_start(k_bytes[32 * quadrant : 32 * quadrant + 4, :].bitcast(I32), keys_scales[0, 4 * quadrant : 4 * quadrant + 4, :].bitcast(I32))
-        nc.vector.memset(v_bytes[0:64, :].bitcast(I32), 0)
-        nc.vector.memset(v_bytes[96:128, :].bitcast(I32), 0)
-
-        warm = keep.tile([P, 2], F32, name="warm")
-        nc.vector.memset(warm[:, 0:1], 0.0)
-        nc.scalar.activation(warm[:, 1:2], warm[:, 0:1], ACT.Exp)
+        for quadrant in range(P // QUADRANT):
+            nc.sync.dma_start(plane_rows(k_bytes, quadrant), keys_scales[0, BLOCKS * quadrant : BLOCKS * (quadrant + 1), :].bitcast(I32))
+        nc.vector.memset(v_bytes[0:PARKED, :].bitcast(I32), 0)
 
         k_words = load_words(keys_words, "k_words")
         size_col = keep.tile([P, 2, 8], F32, name="size_col")
@@ -81,9 +83,12 @@ def tile_attend_bspanread_s_kernel(tc, query, keys_words, keys_scales, gout, val
         ident = keep.tile([P, P], F32, name="ident")
         make_identity(nc, ident[:])
 
-        def quantise(raw, name):
-            grouped = keep.tile([P, Q, PACK], BF16, name=name + "_grouped", align_bytes=64)
-            nc.scalar.copy(grouped[:], raw[:].rearrange("p j q -> p q j"))
+        def interleave(raw, name):
+            grouped = keep.tile([P, Q, PACK], BF16, name=name, align_bytes=64)
+            nc.scalar.activation(grouped[:], raw[:].rearrange("p j q -> p q j"), ACT.Copy)
+            return grouped
+
+        def quantise(grouped, name):
             codes = keep.tile([P, Q], U32, name=name + "_codes", align_bytes=64)
             scales = keep.tile([P, Q], U8, name=name + "_scales", align_bytes=64)
             nc.vector.quantize_mx(out=codes[:].bitcast(FP8X4), scales=scales[:], in_=grouped[:].rearrange("p q j -> p (q j)"))
@@ -91,47 +96,64 @@ def tile_attend_bspanread_s_kernel(tc, query, keys_words, keys_scales, gout, val
 
         v_rows = keep.tile([P, I], U8, name="v_rows", align_bytes=64)
         nc.vector.tensor_copy(v_rows[:], v_bytes[:].indirect(offsets[:]))
-        v_scale = keep.tile([P, I], U8, name="v_scale", align_bytes=64)
-        for quadrant in range(4):
-            at = 64 + 8 * quadrant
-            nc.sync.dma_start(v_scale[32 * quadrant : 32 * quadrant + 4, :].bitcast(I32), v_rows[at : at + 8 : 2, :].bitcast(I32))
+        v_plane = keep.tile([P, I], U8, name="v_plane", align_bytes=64)
+        for quadrant in range(P // QUADRANT):
+            first = PARKED + BLOCKS * quadrant
+            nc.sync.dma_start(plane_rows(v_plane, quadrant), v_rows[first : first + BLOCKS, :].bitcast(I32))
 
-        k_scale = keep.tile([P, I], U8, name="k_scale", align_bytes=64)
-        nc.vector.tensor_copy(k_scale[:], k_bytes[:].indirect(offsets[:]))
+        k_plane = keep.tile([P, I], U8, name="k_plane", align_bytes=64)
+        nc.vector.tensor_copy(k_plane[:], k_bytes[:].indirect(offsets[:]))
         old_rows = keep.tile([P, T], F32, name="old_rows", tag="keys_then_old", align_bytes=64)
         nc.sync.dma_start(old_rows[:], old)
-        q_codes, q_scales = quantise(q_raw, "q")
+        q_codes, q_scales = quantise(interleave(q_raw, "q_grouped"), "q")
 
         key_banks = [psum.tile([P, I], F32, name="key_bank%d" % h) for h in range(2)]
         for h in range(2):
             for e in range(2):
                 nc.tensor.transpose(key_banks[h][:, HALF + e * P : HALF + (e + 1) * P], size_col[:, h, e : e + 1].to_broadcast([P, P]), ident[:])
 
-        def product(bank, words, picked, scale, codes, scales, h):
+        def product(sums, words, picked, plane, codes, scales, h):
             nc.vector.tensor_copy(picked[:, slots(h)], words[:].indirect(listed(h)))
-            nc.tensor.matmul_mx(out=bank, lhsT=codes[:].bitcast(FP8X4), lhsT_scale=scales[:], rhs=picked[:, slots(h)].bitcast(FP8X4), rhs_scale=scale[:, slots(h)], start=True, stop=True)
-            return bank
+            nc.tensor.matmul_mx(
+                out=sums,
+                lhsT=codes[:].bitcast(FP8X4),
+                lhsT_scale=scales[:],
+                rhs=picked[:, slots(h)].bitcast(FP8X4),
+                rhs_scale=plane[:, slots(h)],
+                start=True,
+                stop=True,
+            )
+            return sums
 
         k_picked = keep.tile([P, I], U32, name="k_picked", align_bytes=64)
-        a = [product(key_banks[h][:, 0:HALF], k_words, k_picked, k_scale, q_codes, q_scales, h) for h in range(2)]
-
-        g_codes, g_scales = quantise(g_raw, "g")
+        a = [product(key_banks[h][:, 0:HALF], k_words, k_picked, k_plane, q_codes, q_scales, h) for h in range(2)]
+        g_grouped = interleave(g_raw, "g_grouped")
 
         th = keep.tile([P, I], F32, name="th")
         span_sum = keep.tile([P, G], F32, name="span_sum")
-        size_row = keep.tile([P, I], F32, name="size_row")
-        gate = keep.tile([P, I], F32, name="gate")
-        weight = keep.tile([P, I], F32, name="weight")
         for h in range(2):
             nc.vector.tensor_reduce(span_sum[:, spans(h)], by_span(a[h]), AX.X, ALU.add)
             nc.scalar.activation(th[:, slots(h)], a[h], ACT.Tanh, scale=0.5)
-            nc.scalar.copy(size_row[:, slots(h)].rearrange("p (n e) -> p n e", e=2), key_banks[h][:, HALF:I].rearrange("p (e n) -> p n e", e=2))
-            nc.scalar.activation(gate[:, slots(h)], th[:, slots(h)], ACT.Copy, bias=1.0, scale=1.0)
-            nc.gpsimd.tensor_tensor(weight[:, slots(h)], gate[:, slots(h)], size_row[:, slots(h)], ALU.mult)
+        g_codes, g_scales = quantise(g_grouped, "g")
 
+        weight = keep.tile([P, I], F32, name="weight")
+
+        def weigh(h):
+            size_half = key_banks[h][:, HALF:I].rearrange("p (e n) -> p n e", e=2)
+            nc.vector.scalar_tensor_tensor(
+                weight[:, slots(h)].rearrange("p (n e) -> p n e", e=2),
+                th[:, slots(h)].rearrange("p (n e) -> p n e", e=2),
+                1.0,
+                size_half,
+                ALU.add,
+                ALU.mult,
+            )
+
+        weigh(0)
         neg_s = keep.tile([P, G], F32, name="neg_s")
         neg_max = keep.tile([P, 1], F32, name="neg_max")
         nc.vector.tensor_scalar(neg_s[:], span_sum[:], -1.0 / SPAN, None, ALU.mult, ALU.min, accum_out=neg_max[:])
+        weigh(1)
         p = keep.tile([P, G], F32, name="p")
         z = keep.tile([P, 1], F32, name="z")
         nc.scalar.activation(p[:], neg_s[:], ACT.Exp, bias=neg_max[:], scale=-1.0, accum_out=z[:])
@@ -140,7 +162,7 @@ def tile_attend_bspanread_s_kernel(tc, query, keys_words, keys_scales, gout, val
 
         v_picked = keep.tile([P, I], U32, name="v_picked", align_bytes=64)
         val_banks = [psum.tile([P, HALF], F32, name="val_bank%d" % h) for h in range(2)]
-        c0 = [product(val_banks[h][:], v_words, v_picked, v_scale, g_codes, g_scales, h) for h in range(2)]
+        c0 = [product(val_banks[h][:], v_words, v_picked, v_plane, g_codes, g_scales, h) for h in range(2)]
 
         inv_z = keep.tile([P, 1], F32, name="inv_z", tag="v_words", align_bytes=64)
         nc.vector.reciprocal(inv_z[:], z[:])
@@ -162,15 +184,16 @@ def tile_attend_bspanread_s_kernel(tc, query, keys_words, keys_scales, gout, val
         grad = keep.tile([P, I], F32, name="grad")
         for h in range(2):
             nc.vector.scalar_tensor_tensor(by_span(grad[:, slots(h)]), spread(u_span[:, spans(h)]), mean[:], by_span(own[:, slots(h)]), ALU.subtract, ALU.add)
+
         window = keep.tile([P, T], F32, name="window")
-        for at in range(0, T, 512):
-            nc.gpsimd.memset(window[:, at : at + 512], 0.0)
+        for first in range(0, T, CLEAR_WIDTH):
+            nc.gpsimd.memset(window[:, first : first + CLEAR_WIDTH], 0.0)
         nc.vector.tensor_tensor(window[:].indirect(offsets[:]), grad[:], share[:], ALU.mult)
 
-        at = 0
+        done = 0
         for n, width in enumerate(STORE_WIDTHS):
-            cols = slice(at, at + width)
+            cols = slice(done, done + width)
             total = keep.tile([P, width], F32, name="total%d" % n)
             nc.vector.tensor_tensor(total[:], window[:, cols], old_rows[:, cols], ALU.add)
             nc.sync.dma_start(out[:, cols], total[:])
-            at = at + width
+            done = done + width

from contextlib import ExitStack

import concourse.mybir as mybir
from concourse.masks import make_identity

D, E, T, I, Q, G = 512, 512, 2048, 512, 128, 64
FLOPS = 2 * Q * I * (D + E)

F32 = mybir.dt.float32
BF16 = mybir.dt.bfloat16
I32 = mybir.dt.int32
U32 = mybir.dt.uint32
U16 = mybir.dt.uint16
U8 = mybir.dt.uint8
FP8X4 = mybir.dt.float8_e4m3fn_x4
ALU = mybir.AluOpType
ACT = mybir.ActivationFunctionType
AX = mybir.AxisListType

P = 128
PACK = 4
SPAN = I // G
HALF = I // 2
QUADRANT = 32
BLOCKS = 4
PARKED = P - 16
CLEAR_WIDTH = 512
STORE_WIDTHS = (256, 512, 512, 512, 256)


def tile_attend_bspanread_s_kernel(tc, query, keys_words, keys_scales, gout, vals_words, vals_scales, size, old, offs, out):
    nc = tc.nc
    with ExitStack() as ctx:
        keep = ctx.enter_context(tc.tile_pool(name="keep", bufs=1))
        psum = ctx.enter_context(tc.psum_pool(name="psum", bufs=1))

        def slots(h):
            return slice(h * HALF, (h + 1) * HALF)

        def spans(h):
            return slice(h * (G // 2), (h + 1) * (G // 2))

        def by_span(ap):
            return ap.rearrange("p (g j) -> p g j", j=SPAN)

        def spread(ap):
            return ap.unsqueeze(2).to_broadcast([P, ap.shape[1], SPAN])

        def plane_rows(plane, quadrant):
            return plane[QUADRANT * quadrant : QUADRANT * quadrant + BLOCKS, :].bitcast(I32)

        def load_rows(rows, name):
            raw = keep.tile([P, PACK, Q], F32, name=name)
            nc.sync.dma_start(raw[:], rows.rearrange("(p j) q -> p j q", j=PACK))
            return raw

        def load_words(words, name):
            tile = keep.tile([P, T], U32, name=name, tag=name, align_bytes=64)
            nc.sync.dma_start(tile[:].bitcast(I32), words[0].rearrange("p n t -> p (n t)").bitcast(I32))
            return tile

        offsets = keep.tile([P, I // 16], U16, name="offsets")
        nc.sync.dma_start(offsets[:], offs)

        def listed(h):
            return offsets[:, h * (HALF // 16) : (h + 1) * (HALF // 16)]

        k_bytes = keep.tile([P, T], U8, name="k_bytes", tag="keys_then_old", align_bytes=64)
        nc.vector.memset(k_bytes[:].bitcast(I32), 0)
        v_bytes = keep.tile([P, T], U8, name="v_bytes", align_bytes=64)
        nc.sync.dma_start(v_bytes[PARKED:P, :].bitcast(I32), vals_scales[0].bitcast(I32))
        q_raw = load_rows(query, "q_raw")
        for quadrant in range(P // QUADRANT):
            nc.sync.dma_start(plane_rows(k_bytes, quadrant), keys_scales[0, BLOCKS * quadrant : BLOCKS * (quadrant + 1), :].bitcast(I32))
        nc.vector.memset(v_bytes[0:PARKED, :].bitcast(I32), 0)

        k_words = load_words(keys_words, "k_words")
        size_col = keep.tile([P, 2, 8], F32, name="size_col")
        nc.sync.dma_start(size_col[:, :, 0:2], size[0].rearrange("(h p e) -> p h e", h=2, e=2))
        g_raw = load_rows(gout, "g_raw")
        v_words = load_words(vals_words, "v_words")

        ident = keep.tile([P, P], F32, name="ident")
        make_identity(nc, ident[:])

        def interleave(raw, name):
            grouped = keep.tile([P, Q, PACK], BF16, name=name, align_bytes=64)
            nc.scalar.activation(grouped[:], raw[:].rearrange("p j q -> p q j"), ACT.Copy)
            return grouped

        def quantise(grouped, name):
            codes = keep.tile([P, Q], U32, name=name + "_codes", align_bytes=64)
            scales = keep.tile([P, Q], U8, name=name + "_scales", align_bytes=64)
            nc.vector.quantize_mx(out=codes[:].bitcast(FP8X4), scales=scales[:], in_=grouped[:].rearrange("p q j -> p (q j)"))
            return codes, scales

        v_rows = keep.tile([P, I], U8, name="v_rows", align_bytes=64)
        nc.vector.tensor_copy(v_rows[:], v_bytes[:].indirect(offsets[:]))
        v_plane = keep.tile([P, I], U8, name="v_plane", align_bytes=64)
        for quadrant in range(P // QUADRANT):
            first = PARKED + BLOCKS * quadrant
            nc.sync.dma_start(plane_rows(v_plane, quadrant), v_rows[first : first + BLOCKS, :].bitcast(I32))

        k_plane = keep.tile([P, I], U8, name="k_plane", align_bytes=64)
        nc.vector.tensor_copy(k_plane[:], k_bytes[:].indirect(offsets[:]))
        old_rows = keep.tile([P, T], F32, name="old_rows", tag="keys_then_old", align_bytes=64)
        nc.sync.dma_start(old_rows[:], old)
        q_codes, q_scales = quantise(interleave(q_raw, "q_grouped"), "q")

        key_banks = [psum.tile([P, I], F32, name="key_bank%d" % h) for h in range(2)]
        for h in range(2):
            for e in range(2):
                nc.tensor.transpose(key_banks[h][:, HALF + e * P : HALF + (e + 1) * P], size_col[:, h, e : e + 1].to_broadcast([P, P]), ident[:])

        def product(sums, words, picked, plane, codes, scales, h):
            nc.vector.tensor_copy(picked[:, slots(h)], words[:].indirect(listed(h)))
            nc.tensor.matmul_mx(
                out=sums,
                lhsT=codes[:].bitcast(FP8X4),
                lhsT_scale=scales[:],
                rhs=picked[:, slots(h)].bitcast(FP8X4),
                rhs_scale=plane[:, slots(h)],
                start=True,
                stop=True,
            )
            return sums

        k_picked = keep.tile([P, I], U32, name="k_picked", align_bytes=64)
        a = [product(key_banks[h][:, 0:HALF], k_words, k_picked, k_plane, q_codes, q_scales, h) for h in range(2)]
        g_grouped = interleave(g_raw, "g_grouped")

        th = keep.tile([P, I], F32, name="th")
        span_sum = keep.tile([P, G], F32, name="span_sum")
        for h in range(2):
            nc.vector.tensor_reduce(span_sum[:, spans(h)], by_span(a[h]), AX.X, ALU.add)
            nc.scalar.activation(th[:, slots(h)], a[h], ACT.Tanh, scale=0.5)
        g_codes, g_scales = quantise(g_grouped, "g")

        weight = keep.tile([P, I], F32, name="weight")

        def weigh(h):
            size_half = key_banks[h][:, HALF:I].rearrange("p (e n) -> p n e", e=2)
            nc.vector.scalar_tensor_tensor(
                weight[:, slots(h)].rearrange("p (n e) -> p n e", e=2),
                th[:, slots(h)].rearrange("p (n e) -> p n e", e=2),
                1.0,
                size_half,
                ALU.add,
                ALU.mult,
            )

        weigh(0)
        neg_s = keep.tile([P, G], F32, name="neg_s")
        neg_max = keep.tile([P, 1], F32, name="neg_max")
        nc.vector.tensor_scalar(neg_s[:], span_sum[:], -1.0 / SPAN, None, ALU.mult, ALU.min, accum_out=neg_max[:])
        weigh(1)
        p = keep.tile([P, G], F32, name="p")
        z = keep.tile([P, 1], F32, name="z")
        nc.scalar.activation(p[:], neg_s[:], ACT.Exp, bias=neg_max[:], scale=-1.0, accum_out=z[:])
        rest = keep.tile([P, I], F32, name="rest")
        nc.scalar.activation(rest[:], th[:], ACT.Copy, bias=4.0, scale=-4.0)

        v_picked = keep.tile([P, I], U32, name="v_picked", align_bytes=64)
        val_banks = [psum.tile([P, HALF], F32, name="val_bank%d" % h) for h in range(2)]
        c0 = [product(val_banks[h][:], v_words, v_picked, v_plane, g_codes, g_scales, h) for h in range(2)]

        inv_z = keep.tile([P, 1], F32, name="inv_z", tag="v_words", align_bytes=64)
        nc.vector.reciprocal(inv_z[:], z[:])
        share = keep.tile([P, I], F32, name="share")
        nc.scalar.activation(by_span(share[:]), spread(p[:]), ACT.Copy, scale=inv_z[:])

        u = keep.tile([P, I], F32, name="u")
        u_span = keep.tile([P, G], F32, name="u_span")
        own = keep.tile([P, I], F32, name="own")
        for h in range(2):
            nc.vector.scalar_tensor_tensor(u[:, slots(h)], c0[h], 4.0, weight[:, slots(h)], ALU.mult, ALU.mult)
        for h in range(2):
            nc.vector.tensor_reduce(u_span[:, spans(h)], by_span(u[:, slots(h)]), AX.X, ALU.add)
        nc.vector.tensor_tensor(own[:, slots(0)], u[:, slots(0)], rest[:, slots(0)], ALU.mult)
        weighed = keep.tile([P, G], F32, name="weighed")
        mean = keep.tile([P, 1], F32, name="mean")
        nc.vector.scalar_tensor_tensor(weighed[:], u_span[:], inv_z[:], p[:], ALU.mult, ALU.mult, accum_out=mean[:])
        nc.vector.tensor_tensor(own[:, slots(1)], u[:, slots(1)], rest[:, slots(1)], ALU.mult)
        grad = keep.tile([P, I], F32, name="grad")
        for h in range(2):
            nc.vector.scalar_tensor_tensor(by_span(grad[:, slots(h)]), spread(u_span[:, spans(h)]), mean[:], by_span(own[:, slots(h)]), ALU.subtract, ALU.add)

        window = keep.tile([P, T], F32, name="window")
        for first in range(0, T, CLEAR_WIDTH):
            nc.gpsimd.memset(window[:, first : first + CLEAR_WIDTH], 0.0)
        nc.vector.tensor_tensor(window[:].indirect(offsets[:]), grad[:], share[:], ALU.mult)

        done = 0
        for n, width in enumerate(STORE_WIDTHS):
            cols = slice(done, done + width)
            total = keep.tile([P, width], F32, name="total%d" % n)
            nc.vector.tensor_tensor(total[:], window[:, cols], old_rows[:, cols], ALU.add)
            nc.sync.dma_start(out[:, cols], total[:])
            done = done + width
